import numpy as np
import ml_dtypes


def mxq(x, axis, fmt="e4m3"):
    dtype, down = {"e4m3": (ml_dtypes.float8_e4m3fn, 7), "e5m2": (ml_dtypes.float8_e5m2, 14)}[fmt]
    v = np.moveaxis(np.asarray(x, np.float32).astype(ml_dtypes.bfloat16).astype(np.float64), axis, -1)
    blocks = v.reshape(v.shape[:-1] + (-1, 32))
    amax = np.abs(blocks).max(-1, keepdims=True)
    byte = np.maximum(np.where(amax > 0, np.frexp(amax)[1] - 1 + 127, 0) - down, 1)
    scale = np.exp2(byte - 127.0)
    codes = (blocks / scale).astype(np.float32).astype(dtype).astype(np.float64)
    return np.moveaxis((codes * scale).reshape(v.shape), -1, axis)


WIDE = False


def mx_kscale(k):
    if not WIDE:
        return np.ones(k)
    levels = np.array([10, -10, 5, -5, 0])
    if k % 512:
        return np.exp2(np.random.permutation(np.resize(levels, k // 32))).repeat(32)
    a = np.empty((k // 512, 16))
    for p in range(k // 512):
        a[p, :8] = np.random.permutation(np.resize(levels, 8))
        for g in range(8):
            far = levels[np.abs(levels - a[p, g]) >= 10]
            a[p, g + 8] = far[np.random.randint(len(far))]
    return np.exp2(a.ravel()).repeat(32)


def f64(x):
    return np.asarray(x).astype(np.float64)


def striped(idx):
    return np.tile(idx.reshape(-1, 16).T, (8, 1)).astype(np.uint16)


def unstriped(offs):
    return offs[:16].T.reshape(-1).astype(np.int64)


E2M1 = np.array([0.0, 0.5, 1.0, 1.5, 2.0, 3.0, 4.0, 6.0, -0.0, -0.5, -1.0, -1.5, -2.0, -3.0, -4.0, -6.0])


def pack_weight(w, fmt):
    k, n = w.shape
    w = f64(np.asarray(w, np.float32).astype(ml_dtypes.bfloat16)).reshape(k // 32, 32, n)
    amax = np.abs(w).max(1)
    if fmt == "e4m3":
        byte = np.frexp(amax)[1] - 1 + 127 - 7
    else:
        mant, ex = np.frexp(amax / 6.0)
        byte = np.where(mant > 0.5, ex, ex - 1) + 127
    byte = np.clip(np.where(amax > 0, byte, 1), 1, 254)
    scaled = (w * np.exp2(127.0 - byte)[:, None, :]).reshape(k, n).astype(np.float32)
    by_word = np.ascontiguousarray(scaled.reshape(k // 512, 128, 4, n).transpose(0, 1, 3, 2))
    if fmt == "e4m3":
        words = by_word.astype(ml_dtypes.float8_e4m3fn).view(np.uint8)
    else:
        c = by_word.astype(ml_dtypes.float4_e2m1fn).view(np.uint8) & 0xF
        words = (c[..., 0::2] | (c[..., 1::2] << 4)).reshape(k // 512, 128, 2 * n)
    return np.ascontiguousarray(words), np.ascontiguousarray(byte.astype(np.uint8).reshape(k // 512, 16, n))


def unpack_weight(words, scales, fmt):
    g, _, n = scales.shape
    words = np.ascontiguousarray(words).reshape(g, 128, n, -1)
    if fmt == "e4m3":
        vals = words.view(ml_dtypes.float8_e4m3fn).astype(np.float64)
    else:
        nib = np.empty((g, 128, n, 4), np.uint8)
        nib[..., 0::2] = words & 0xF
        nib[..., 1::2] = words >> 4
        vals = E2M1[nib]
    vals = vals * np.repeat(np.exp2(scales.astype(np.float64) - 127.0), 8, axis=1)[..., None]
    return vals.transpose(0, 1, 3, 2).reshape(g * 512, n)


def gelu(v):
    return 0.5 * v * (1.0 + np.tanh(np.sqrt(2.0 / np.pi) * (v + 0.044715 * v**3)))


def striped8(idx):
    return np.concatenate([v.reshape(-1, 16).T for v in idx]).astype(np.uint16)


def unstriped8(offs):
    return np.stack([offs[16 * g:16 * g + 16].T.reshape(-1) for g in range(8)]).astype(np.int64)


def runs(v, idx8):
    k = np.arange(v.shape[0])
    return v[k[:, None], idx8[k % 512 // 64]]


def often(T, S):
    return np.random.permutation(T)[(T * np.random.uniform(0, 1, S) ** 4).astype(np.int64)]


K, T, S, H, P, N = 1024, 2048, 1024, 1024, 512, 768

def setup_inputs():
    n = np.random.standard_normal
    s = mx_kscale(K)[:, None]
    u = mx_kscale(H)[:, None]
    d = {}
    d["tab_words"], d["tab_scales"] = pack_weight(n((K, T)) * s, "e4m3")
    d["offs"] = striped8(np.stack([often(T, S) for _ in range(8)]))
    d["w1"] = (0.55 * n((K, H)) / s / K ** 0.5).astype(np.float32)
    d["gain"] = (np.exp(0.3 * n(H)) * u[:, 0]).astype(np.float32)
    d["pos1"] = striped(np.random.permutation(S)[:P])
    d["pos2"] = striped(np.random.permutation(S)[:P])
    d["shelter"] = np.exp(0.4 * n((H, P))).astype(np.float32)
    d["w4_words"], d["w4_scales"] = pack_weight(1.3 * n((H, N)) / u / H ** 0.5, "e2m1")
    d["least"] = (0.5 * n(N) - 0.4).astype(np.float32)
    return d

def reference(tab_words, tab_scales, offs, w1, gain, pos1, pos2, shelter, w4_words, w4_scales, least):
    v = runs(unpack_weight(tab_words, tab_scales, "e4m3"), unstriped8(offs))
    ph = mxq(f64(w1), 0, "e4m3").T @ v
    h = (np.sin(ph) + np.cos(ph)) * f64(gain)[:, None]
    x = h[:, unstriped(pos1)] - f64(shelter) * h[:, unstriped(pos2)]
    w4 = unpack_weight(w4_words, w4_scales, "e2m1")
    y = w4.T @ mxq(x, 0, "e4m3")
    return np.maximum(y, f64(least)[:, None])

@@ -1,0 +1,243 @@
+import math
+from contextlib import ExitStack
+
+import concourse.mybir as mybir
+
+K, T, S, H, M, N = 1024, 2048, 1024, 1024, 512, 768
+FLOPS = 2 * K * H * S + 2 * H * N * M
+
+F32 = mybir.dt.float32
+BF16 = mybir.dt.bfloat16
+I32 = mybir.dt.int32
+U32 = mybir.dt.uint32
+U16 = mybir.dt.uint16
+U8 = mybir.dt.uint8
+FP8X4 = mybir.dt.float8_e4m3fn_x4
+FP4X4 = mybir.dt.float4_e2m1fn_x4
+ALU = mybir.AluOpType
+ACT = mybir.ActivationFunctionType
+
+P = 128
+PACK = 4
+PASS = P * PACK
+BANK = 512
+W_CHUNK = 256
+
+
+def tile_list_drift_fence_advisory_kernel(
+    tc, tab_words, tab_scales, offs, w1, gain, pos1, pos2, shelter, w4_words, w4_scales, least, out
+):
+    nc = tc.nc
+    with ExitStack() as ctx:
+        lists = ctx.enter_context(tc.tile_pool(name="lists", bufs=1))
+        keep = ctx.enter_context(tc.tile_pool(name="keep", bufs=1))
+        ring = ctx.enter_context(tc.tile_pool(name="ring", bufs=3))
+        psum = ctx.enter_context(tc.psum_pool(name="psum", bufs=1))
+
+        warm_in = keep.tile([P, 1], F32)
+        warm_out = keep.tile([P, 1], F32)
+        tab_bytes = keep.tile([P, T], U8, align_bytes=64)
+        nc.vector.memset(tab_bytes[:].bitcast(I32), 0)
+        nc.gpsimd.memset(warm_in[:], 0.0)
+        nc.scalar.activation(out=warm_out[:], in_=warm_in[:], func=ACT.Sin)
+        w4_sc = keep.tile([P, 2, N], U8, align_bytes=64)
+        nc.gpsimd.memset(w4_sc[:].rearrange("p a n -> p (a n)").bitcast(I32), 0)
+
+        offs_sb = lists.tile([P, S // 16], U16)
+        nc.sync.dma_start(offs_sb[:], offs)
+        for a in range(2):
+            for e in range(2):
+                nc.sync.dma_start(
+                    out=tab_bytes[4 * a + e : P : 16, :].bitcast(I32),
+                    in_=tab_scales[a, e:16:2, :].bitcast(I32),
+                )
+
+        tab_sb = []
+        w_raw = {}
+
+        def load_table(a):
+            buf = keep.tile([P, T], U32, name="tab%d" % a, align_bytes=64)
+            nc.sync.dma_start(
+                out=buf[:].bitcast(I32), in_=tab_words[a].rearrange("p n i -> p (n i)").bitcast(I32)
+            )
+            tab_sb.append(buf)
+
+        def load_w1(a, b):
+            for c in range(PASS // W_CHUNK):
+                buf = keep.tile([P, PACK, W_CHUNK], F32, name="wraw%d%d%d" % (a, b, c))
+                c0 = PASS * b + W_CHUNK * c
+                nc.sync.dma_start(
+                    out=buf[:],
+                    in_=w1[PASS * a : PASS * (a + 1), c0 : c0 + W_CHUNK].rearrange("(p j) c -> p j c", j=PACK),
+                )
+                w_raw[(a, b, c)] = buf
+
+        w_bf = {}
+        w_codes = {}
+        w_scales = {}
+
+        def round_w1(a, b, c, copy):
+            if (a, b) not in w_bf:
+                w_bf[(a, b)] = keep.tile([P, PACK, P, PACK], BF16, name="wbf%d%d" % (a, b), align_bytes=64)
+            per = W_CHUNK // PACK
+            copy(
+                out=w_bf[(a, b)][:, :, per * c : per * (c + 1), :].rearrange("p t m j -> p m t j"),
+                in_=w_raw[(a, b, c)][:].rearrange("p j (m t) -> p m t j", t=PACK),
+            )
+
+        def quantise_w1(a, b):
+            codes = keep.tile([P, PASS], U32, name="wcodes%d%d" % (a, b), align_bytes=64)
+            scales = keep.tile([P, PASS], U8, name="wscales%d%d" % (a, b), align_bytes=64)
+            nc.vector.quantize_mx(
+                out=codes[:].bitcast(FP8X4),
+                scales=scales[:],
+                in_=w_bf[(a, b)][:].rearrange("p t m j -> p (t m j)"),
+            )
+            w_codes[(a, b)] = codes
+            w_scales[(a, b)] = scales
+
+        load_table(0)
+        load_w1(0, 0)
+        load_table(1)
+        load_w1(1, 0)
+
+        picked_bytes = keep.tile([P, S], U8, align_bytes=64)
+        nc.vector.tensor_copy(out=picked_bytes[:], in_=tab_bytes[:].indirect(offs_sb[:]))
+        v_scales = keep.tile([P, S], U8, align_bytes=64)
+        nc.vector.tensor_copy(out=v_scales[:].bitcast(I32), in_=picked_bytes[:].bitcast(I32))
+        for a in range(2):
+            for e in range(2):
+                nc.sync.dma_start(
+                    out=v_scales[4 * a + 2 + e : P : 32, :].bitcast(I32),
+                    in_=picked_bytes[16 + 4 * a + e : P : 32, :].bitcast(I32),
+                )
+
+        v_codes = []
+        for a in range(2):
+            picked = keep.tile([P, S], U32, name="picked%d" % a, align_bytes=64)
+            nc.vector.tensor_copy(out=picked[:], in_=tab_sb[a][:].indirect(offs_sb[:]))
+            v_codes.append(picked)
+            round_w1(a, 0, 0, nc.scalar.copy)
+            round_w1(a, 0, 1, nc.scalar.copy if a == 0 else nc.vector.tensor_copy)
+            quantise_w1(a, 0)
+
+        pos1_sb = lists.tile([P, M // 16], U16)
+        pos2_sb = lists.tile([P, M // 16], U16)
+        gain_sb = keep.tile([P, 2, PACK], F32)
+        shelter_sb = {}
+
+        def load_shelter(b, t0):
+            buf = keep.tile([P, 2, M], F32, name="shelter%d%d" % (b, t0))
+            rows = shelter[PASS * b : PASS * (b + 1), :].rearrange("(p t) m -> p t m", t=PACK)
+            nc.sync.dma_start(out=buf[:], in_=rows[:, t0 : t0 + 2, :])
+            shelter_sb[(b, t0)] = buf[:, 0, :]
+            shelter_sb[(b, t0 + 1)] = buf[:, 1, :]
+
+        load_w1(0, 1)
+        nc.sync.dma_start(pos2_sb[:], pos2)
+        nc.sync.dma_start(pos1_sb[:], pos1)
+        load_shelter(0, 0)
+        nc.sync.dma_start(out=gain_sb[:], in_=gain.rearrange("(b p t) -> p b t", b=2, t=PACK))
+        load_w1(1, 1)
+        load_shelter(0, 2)
+        load_shelter(1, 0)
+        load_shelter(1, 2)
+        w4_sb = keep.tile([P, 2, 2 * N], U8, align_bytes=64)
+        for a in range(2):
+            nc.sync.dma_start(out=w4_sb[:, a, :].bitcast(I32), in_=w4_words[a].bitcast(I32))
+        for q in range(4):
+            nc.sync.dma_start(
+                out=w4_sc[32 * q : 32 * q + 4, :, :].bitcast(I32),
+                in_=w4_scales[:, 4 * q : 4 * q + 4, :].rearrange("a r n -> r a n").bitcast(I32),
+            )
+        least_sb = keep.tile([P, N // P], F32)
+        with nc.allow_non_contiguous_dma(reason="one floor for each output row, rows on partitions"):
+            nc.sync.dma_start(out=least_sb[:], in_=least.rearrange("(j p) -> p j", p=P))
+
+        round_w1(0, 1, 0, nc.vector.tensor_copy)
+        round_w1(0, 1, 1, nc.vector.tensor_copy)
+        quantise_w1(0, 1)
+
+        x_rows = [keep.tile([P, PACK, M], BF16, name="xrows%d" % b, align_bytes=64) for b in range(2)]
+        x_codes = [keep.tile([P, M], U32, name="xcodes%d" % b, align_bytes=64) for b in range(2)]
+        x_scales = [keep.tile([P, M], U8, name="xscales%d" % b, align_bytes=64) for b in range(2)]
+
+        def features(b, t):
+            index = PACK * b + t
+            folded = ring.tile([P, S], F32, name="folded")
+            for half in range(2):
+                bank = psum.tile([P, BANK], F32, name="bank%d" % ((2 * index + half) % 8))
+                cols = slice(BANK * half, BANK * (half + 1))
+                for a in range(2):
+                    nc.tensor.matmul_mx(
+                        out=bank[:],
+                        lhsT=w_codes[(a, b)][:, P * t : P * (t + 1)].bitcast(FP8X4),
+                        lhsT_scale=w_scales[(a, b)][:, P * t : P * (t + 1)],
+                        rhs=v_codes[a][:, cols].bitcast(FP8X4),
+                        rhs_scale=v_scales[4 * a : P, cols],
+                        start=(a == 0),
+                        stop=(a == 1),
+                    )
+                nc.scalar.activation(out=folded[:, cols], in_=bank[:], func=ACT.Abs, bias=-math.pi / 4)
+            wave = keep.tile([P, S], F32, name="wave%d" % index)
+            nc.scalar.activation(out=wave[:], in_=folded[:], func=ACT.Sin, scale=-1.0, bias=math.pi / 2)
+            lee = ring.tile([P, M], F32, name="lee")
+            nc.vector.tensor_tensor(lee[:], wave[:].indirect(pos2_sb[:]), shelter_sb[(b, t)], ALU.mult)
+            diff = ring.tile([P, M], F32, name="diff")
+            nc.vector.tensor_tensor(diff[:], wave[:].indirect(pos1_sb[:]), lee[:], ALU.subtract)
+            nc.vector.tensor_scalar(
+                out=x_rows[b][:, t, :],
+                in0=diff[:],
+                scalar1=gain_sb[:, b, t : t + 1],
+                scalar2=math.sqrt(2.0),
+                op0=ALU.mult,
+                op1=ALU.mult,
+            )
+
+        def quantise_x(b, copy):
+            woven = keep.tile([P, M, PACK], BF16, name="woven%d" % b, align_bytes=64)
+            copy(
+                out=woven[:].rearrange("p (c i) t -> p c t i", i=4),
+                in_=x_rows[b][:].rearrange("p t (c i) -> p c t i", i=4),
+            )
+            nc.vector.quantize_mx(
+                out=x_codes[b][:].bitcast(FP8X4),
+                scales=x_scales[b][:],
+                in_=woven[:].rearrange("p m t -> p (m t)"),
+            )
+
+        features(0, 0)
+        features(0, 1)
+        round_w1(1, 1, 0, nc.scalar.copy)
+        round_w1(1, 1, 1, nc.scalar.copy)
+        quantise_w1(1, 1)
+        features(0, 2)
+        features(0, 3)
+        features(1, 0)
+        quantise_x(0, nc.scalar.copy)
+        for t in range(1, PACK):
+            features(1, t)
+
+        sums = [psum.tile([P, M], F32, name="bank%d" % j) for j in range(N // P)]
+
+        def second_product(j, a):
+            nc.tensor.matmul_mx(
+                out=sums[j][:],
+                lhsT=w4_sb[:, a, 2 * P * j : 2 * P * (j + 1)].bitcast(FP4X4),
+                lhsT_scale=w4_sc[:, a, P * j : P * (j + 1)],
+                rhs=x_codes[a][:].bitcast(FP8X4),
+                rhs_scale=x_scales[a][:],
+                start=(a == 0),
+                stop=(a == 1),
+            )
+
+        for j in range(N // P):
+            second_product(j, 0)
+        quantise_x(1, nc.vector.tensor_copy)
+        for j in range(N // P):
+            second_product(j, 1)
+            result = keep.tile([P, M], F32, name="result%d" % j)
+            nc.vector.tensor_scalar(
+                out=result[:], in0=sums[j][:], scalar1=least_sb[:, j : j + 1], scalar2=None, op0=ALU.max
+            )
+            nc.sync.dma_start(out=out[P * j : P * (j + 1), :], in_=result[:])

@@ -21,7 +21,8 @@ P = 128
 PACK = 4
 PASS = P * PACK
 BANK = 512
-W_CHUNK = 256
+HALF = M // 2
+STAGE_BYTES = 66 * 1024
 
 
 def tile_list_drift_fence_advisory_kernel(
@@ -31,44 +32,67 @@ def tile_list_drift_fence_advisory_kernel(
     with ExitStack() as ctx:
         lists = ctx.enter_context(tc.tile_pool(name="lists", bufs=1))
         keep = ctx.enter_context(tc.tile_pool(name="keep", bufs=1))
-        ring = ctx.enter_context(tc.tile_pool(name="ring", bufs=3))
+        stage = ctx.enter_context(tc.tile_pool(name="stage", bufs=1))
+        ring = ctx.enter_context(tc.tile_pool(name="ring", bufs=2))
         psum = ctx.enter_context(tc.psum_pool(name="psum", bufs=1))
 
-        warm_in = keep.tile([P, 1], F32)
-        warm_out = keep.tile([P, 1], F32)
         tab_bytes = keep.tile([P, T], U8, align_bytes=64)
         nc.vector.memset(tab_bytes[:].bitcast(I32), 0)
-        nc.gpsimd.memset(warm_in[:], 0.0)
-        nc.scalar.activation(out=warm_out[:], in_=warm_in[:], func=ACT.Sin)
-        w4_sc = keep.tile([P, 2, N], U8, align_bytes=64)
-        nc.gpsimd.memset(w4_sc[:].rearrange("p a n -> p (a n)").bitcast(I32), 0)
+        ones = stage.tile([P, STAGE_BYTES // 4], F32, offset=0, align_bytes=64)
+        nc.vector.memset(ones[:, 0:1], 1.0)
+        fold_bias = keep.tile([P, 1], F32)
+        wave_bias = keep.tile([P, 1], F32)
+        nc.vector.tensor_scalar(out=fold_bias[:], in0=ones[:, 0:1], scalar1=-math.pi / 4, scalar2=None, op0=ALU.mult)
+        nc.vector.tensor_scalar(out=wave_bias[:], in0=ones[:, 0:1], scalar1=math.pi / 2, scalar2=None, op0=ALU.mult)
+        warm_out = keep.tile([P, 1], F32)
+        nc.scalar.activation(out=warm_out[:], in_=wave_bias[:], func=ACT.Sin, bias=fold_bias[:])
+
+        placed = [0]
+
+        def staged(shape, dtype, size, name):
+            buf = stage.tile(shape, dtype, name=name, offset=placed[-1], align_bytes=64)
+            placed.append(placed[-1] + size)
+            assert placed[-1] <= STAGE_BYTES
+            return buf
+
+        w4_sc = staged([P, 2, N], U8, 2 * N, "w4_sc")
+        nc.vector.memset(w4_sc[:].rearrange("p a n -> p (a n)").bitcast(I32), 0)
 
         offs_sb = lists.tile([P, S // 16], U16)
+        pos1_sb = lists.tile([P, M // 16], U16)
+        pos2_sb = lists.tile([P, M // 16], U16)
         nc.sync.dma_start(offs_sb[:], offs)
-        for a in range(2):
-            for e in range(2):
-                nc.sync.dma_start(
-                    out=tab_bytes[4 * a + e : P : 16, :].bitcast(I32),
-                    in_=tab_scales[a, e:16:2, :].bitcast(I32),
-                )
+        nc.sync.dma_start(pos2_sb[:], pos2)
+        nc.sync.dma_start(pos1_sb[:], pos1)
+        gain_sb = keep.tile([P, 2, PACK], F32)
+        nc.sync.dma_start(out=gain_sb[:], in_=gain.rearrange("(b p t) -> p b t", b=2, t=PACK))
+        rows = tab_scales.rearrange("a (g e) t -> e g a t", e=2)
+        for e in range(2):
+            nc.sync.dma_start(out=tab_bytes[e:P:8, :].bitcast(I32), in_=rows[e].bitcast(I32))
 
         tab_sb = []
         w_raw = {}
 
         def load_table(a):
-            buf = keep.tile([P, T], U32, name="tab%d" % a, align_bytes=64)
-            nc.sync.dma_start(
-                out=buf[:].bitcast(I32), in_=tab_words[a].rearrange("p n i -> p (n i)").bitcast(I32)
-            )
+            buf = staged([P, T], U32, 4 * T, "tab%d" % a)
+            words = tab_words[a].rearrange("p n i -> p (n i)").bitcast(I32)
+            for c in range(2):
+                cols = slice(T // 2 * c, T // 2 * (c + 1))
+                nc.sync.dma_start(out=buf[:, cols].bitcast(I32), in_=words[:, cols])
             tab_sb.append(buf)
 
-        def load_w1(a, b):
-            for c in range(PASS // W_CHUNK):
-                buf = keep.tile([P, PACK, W_CHUNK], F32, name="wraw%d%d%d" % (a, b, c))
-                c0 = PASS * b + W_CHUNK * c
+        def load_w1(a, b, pieces):
+            width = PASS // pieces
+            for c in range(pieces):
+                name = "wraw%d%d%d" % (a, b, c)
+                if (a, b, c) == (0, 0, 0):
+                    buf = keep.tile([P, PACK, width], F32, name=name)
+                else:
+                    buf = staged([P, PACK, width], F32, 4 * PACK * width, name)
+                c0 = PASS * b + width * c
                 nc.sync.dma_start(
                     out=buf[:],
-                    in_=w1[PASS * a : PASS * (a + 1), c0 : c0 + W_CHUNK].rearrange("(p j) c -> p j c", j=PACK),
+                    in_=w1[PASS * a : PASS * (a + 1), c0 : c0 + width].rearrange("(p j) c -> p j c", j=PACK),
                 )
                 w_raw[(a, b, c)] = buf
 
@@ -79,27 +103,27 @@ def tile_list_drift_fence_advisory_kernel(
         def round_w1(a, b, c, copy):
             if (a, b) not in w_bf:
                 w_bf[(a, b)] = keep.tile([P, PACK, P, PACK], BF16, name="wbf%d%d" % (a, b), align_bytes=64)
-            per = W_CHUNK // PACK
+            per = w_raw[(a, b, c)].shape[2] // PACK
             copy(
                 out=w_bf[(a, b)][:, :, per * c : per * (c + 1), :].rearrange("p t m j -> p m t j"),
                 in_=w_raw[(a, b, c)][:].rearrange("p j (m t) -> p m t j", t=PACK),
             )
 
-        def quantise_w1(a, b):
+        def quantise_w1(a, b, cuts=(0, PACK)):
             codes = keep.tile([P, PASS], U32, name="wcodes%d%d" % (a, b), align_bytes=64)
             scales = keep.tile([P, PASS], U8, name="wscales%d%d" % (a, b), align_bytes=64)
-            nc.vector.quantize_mx(
-                out=codes[:].bitcast(FP8X4),
-                scales=scales[:],
-                in_=w_bf[(a, b)][:].rearrange("p t m j -> p (t m j)"),
-            )
+            for t0, t1 in zip(cuts[:-1], cuts[1:]):
+                nc.vector.quantize_mx(
+                    out=codes[:, P * t0 : P * t1].bitcast(FP8X4),
+                    scales=scales[:, P * t0 : P * t1],
+                    in_=w_bf[(a, b)][:, t0:t1].rearrange("p t m j -> p (t m j)"),
+                )
             w_codes[(a, b)] = codes
             w_scales[(a, b)] = scales
 
         load_table(0)
-        load_w1(0, 0)
+        load_w1(0, 0, 2)
         load_table(1)
-        load_w1(1, 0)
 
         picked_bytes = keep.tile([P, S], U8, align_bytes=64)
         nc.vector.tensor_copy(out=picked_bytes[:], in_=tab_bytes[:].indirect(offs_sb[:]))
@@ -108,41 +132,43 @@ def tile_list_drift_fence_advisory_kernel(
         for a in range(2):
             for e in range(2):
                 nc.sync.dma_start(
-                    out=v_scales[4 * a + 2 + e : P : 32, :].bitcast(I32),
-                    in_=picked_bytes[16 + 4 * a + e : P : 32, :].bitcast(I32),
+                    out=v_scales[8 * a + 2 + e : P : 32, :].bitcast(I32),
+                    in_=picked_bytes[16 + 8 * a + e : P : 32, :].bitcast(I32),
                 )
+        load_w1(1, 0, 4)
 
         v_codes = []
-        for a in range(2):
+
+        def pick_words(a):
             picked = keep.tile([P, S], U32, name="picked%d" % a, align_bytes=64)
             nc.vector.tensor_copy(out=picked[:], in_=tab_sb[a][:].indirect(offs_sb[:]))
             v_codes.append(picked)
-            round_w1(a, 0, 0, nc.scalar.copy)
-            round_w1(a, 0, 1, nc.scalar.copy if a == 0 else nc.vector.tensor_copy)
-            quantise_w1(a, 0)
 
-        pos1_sb = lists.tile([P, M // 16], U16)
-        pos2_sb = lists.tile([P, M // 16], U16)
-        gain_sb = keep.tile([P, 2, PACK], F32)
+        pick_words(0)
+        for c in range(2):
+            round_w1(0, 0, c, nc.scalar.copy)
+        quantise_w1(0, 0)
+        pick_words(1)
+        for c in range(4):
+            round_w1(1, 0, c, nc.scalar.copy if c < 3 else nc.vector.tensor_copy)
+        quantise_w1(1, 0, (0, 1, 2, PACK))
+
         shelter_sb = {}
 
         def load_shelter(b, t0):
-            buf = keep.tile([P, 2, M], F32, name="shelter%d%d" % (b, t0))
+            buf = staged([P, 2, M], F32, 8 * M, "shelter%d%d" % (b, t0))
             rows = shelter[PASS * b : PASS * (b + 1), :].rearrange("(p t) m -> p t m", t=PACK)
             nc.sync.dma_start(out=buf[:], in_=rows[:, t0 : t0 + 2, :])
             shelter_sb[(b, t0)] = buf[:, 0, :]
             shelter_sb[(b, t0 + 1)] = buf[:, 1, :]
 
-        load_w1(0, 1)
-        nc.sync.dma_start(pos2_sb[:], pos2)
-        nc.sync.dma_start(pos1_sb[:], pos1)
+        load_w1(0, 1, 2)
         load_shelter(0, 0)
-        nc.sync.dma_start(out=gain_sb[:], in_=gain.rearrange("(b p t) -> p b t", b=2, t=PACK))
-        load_w1(1, 1)
+        load_w1(1, 1, 2)
         load_shelter(0, 2)
         load_shelter(1, 0)
         load_shelter(1, 2)
-        w4_sb = keep.tile([P, 2, 2 * N], U8, align_bytes=64)
+        w4_sb = staged([P, 2, 2 * N], U8, 4 * N, "w4_sb")
         for a in range(2):
             nc.sync.dma_start(out=w4_sb[:, a, :].bitcast(I32), in_=w4_words[a].bitcast(I32))
         for q in range(4):
@@ -150,7 +176,7 @@ def tile_list_drift_fence_advisory_kernel(
                 out=w4_sc[32 * q : 32 * q + 4, :, :].bitcast(I32),
                 in_=w4_scales[:, 4 * q : 4 * q + 4, :].rearrange("a r n -> r a n").bitcast(I32),
             )
-        least_sb = keep.tile([P, N // P], F32)
+        least_sb = staged([P, N // P], F32, 64, "least_sb")
         with nc.allow_non_contiguous_dma(reason="one floor for each output row, rows on partitions"):
             nc.sync.dma_start(out=least_sb[:], in_=least.rearrange("(j p) -> p j", p=P))
 
@@ -158,12 +184,19 @@ def tile_list_drift_fence_advisory_kernel(
         round_w1(0, 1, 1, nc.vector.tensor_copy)
         quantise_w1(0, 1)
 
-        x_rows = [keep.tile([P, PACK, M], BF16, name="xrows%d" % b, align_bytes=64) for b in range(2)]
-        x_codes = [keep.tile([P, M], U32, name="xcodes%d" % b, align_bytes=64) for b in range(2)]
+        amp_sb = keep.tile([P, 2, PACK], F32)
+        nc.vector.tensor_scalar(out=amp_sb[:], in0=gain_sb[:], scalar1=math.sqrt(2.0), scalar2=None, op0=ALU.mult)
+        below_sb = keep.tile([P, N // P], F32)
+        nc.gpsimd.tensor_scalar(out=below_sb[:], in0=least_sb[:], scalar1=-1.0, scalar2=0.0, op0=ALU.mult, op1=ALU.add)
+        x_rows = keep.tile([P, PACK, M], BF16, align_bytes=64)
+        woven = [keep.tile([P, M, PACK], BF16, name="woven%d" % b, align_bytes=64) for b in range(2)]
+        x_codes = {}
         x_scales = [keep.tile([P, M], U8, name="xscales%d" % b, align_bytes=64) for b in range(2)]
 
-        def features(b, t):
-            index = PACK * b + t
+        diffs = []
+
+        def features(index):
+            b, t = divmod(index, PACK)
             folded = ring.tile([P, S], F32, name="folded")
             for half in range(2):
                 bank = psum.tile([P, BANK], F32, name="bank%d" % ((2 * index + half) % 8))
@@ -174,49 +207,68 @@ def tile_list_drift_fence_advisory_kernel(
                         lhsT=w_codes[(a, b)][:, P * t : P * (t + 1)].bitcast(FP8X4),
                         lhsT_scale=w_scales[(a, b)][:, P * t : P * (t + 1)],
                         rhs=v_codes[a][:, cols].bitcast(FP8X4),
-                        rhs_scale=v_scales[4 * a : P, cols],
+                        rhs_scale=v_scales[8 * a : P, cols],
                         start=(a == 0),
                         stop=(a == 1),
                     )
-                nc.scalar.activation(out=folded[:, cols], in_=bank[:], func=ACT.Abs, bias=-math.pi / 4)
-            wave = keep.tile([P, S], F32, name="wave%d" % index)
-            nc.scalar.activation(out=wave[:], in_=folded[:], func=ACT.Sin, scale=-1.0, bias=math.pi / 2)
+                nc.scalar.activation(out=folded[:, cols], in_=bank[:], func=ACT.Abs, bias=fold_bias[:])
+            wave = keep.tile([P, S], F32, name="wave%d" % index, align_bytes=64)
+            width = BANK if index == 0 else S
+            for c0 in range(0, S, width):
+                cols = slice(c0, c0 + width)
+                nc.scalar.activation(out=wave[:, cols], in_=folded[:, cols], func=ACT.Sin, scale=-1.0, bias=wave_bias[:])
             lee = ring.tile([P, M], F32, name="lee")
-            nc.vector.tensor_tensor(lee[:], wave[:].indirect(pos2_sb[:]), shelter_sb[(b, t)], ALU.mult)
-            diff = ring.tile([P, M], F32, name="diff")
-            nc.vector.tensor_tensor(diff[:], wave[:].indirect(pos1_sb[:]), lee[:], ALU.subtract)
-            nc.vector.tensor_scalar(
-                out=x_rows[b][:, t, :],
-                in0=diff[:],
-                scalar1=gain_sb[:, b, t : t + 1],
-                scalar2=math.sqrt(2.0),
-                op0=ALU.mult,
-                op1=ALU.mult,
-            )
+            diff = keep.tile([P, M], F32, name="diff%d" % index)
+            diffs.append(diff)
+            for h in range(2):
+                cols = slice(HALF * h, HALF * (h + 1))
+                entries = pos2_sb[:, HALF // 16 * h : HALF // 16 * (h + 1)]
+                nc.vector.tensor_tensor(lee[:, cols], wave[:].indirect(entries), shelter_sb[(b, t)][:, cols], ALU.mult)
+            for h in range(2):
+                cols = slice(HALF * h, HALF * (h + 1))
+                entries = pos1_sb[:, HALF // 16 * h : HALF // 16 * (h + 1)]
+                nc.vector.tensor_tensor(diff[:, cols], wave[:].indirect(entries), lee[:, cols], ALU.subtract)
 
-        def quantise_x(b, copy):
-            woven = keep.tile([P, M, PACK], BF16, name="woven%d" % b, align_bytes=64)
-            copy(
-                out=woven[:].rearrange("p (c i) t -> p c t i", i=4),
-                in_=x_rows[b][:].rearrange("p t (c i) -> p c t i", i=4),
-            )
+        def apply_gain(index):
+            b, t = divmod(index, PACK)
+            diff = diffs[index]
+            factor = amp_sb[:, b, t : t + 1]
+            if b == 0:
+                nc.scalar.activation(out=x_rows[:, t, :], in_=diff[:], func=ACT.Copy, scale=factor)
+            elif t < 2:
+                nc.scalar.activation(out=woven[1][:, :, t], in_=diff[:], func=ACT.Copy, scale=factor)
+            else:
+                for h in range(2):
+                    cols = slice(HALF * h, HALF * (h + 1))
+                    nc.vector.tensor_scalar(
+                        out=woven[1][:, cols, t], in0=diff[:, cols], scalar1=factor, scalar2=None, op0=ALU.mult
+                    )
+
+        def quantise_x(b, name):
+            x_codes[b] = keep.tile([P, M], U32, name=name, align_bytes=64)
             nc.vector.quantize_mx(
                 out=x_codes[b][:].bitcast(FP8X4),
                 scales=x_scales[b][:],
-                in_=woven[:].rearrange("p m t -> p (m t)"),
+                in_=woven[b][:].rearrange("p m t -> p (m t)"),
             )
 
-        features(0, 0)
-        features(0, 1)
+        features(0)
+        features(1)
         round_w1(1, 1, 0, nc.scalar.copy)
         round_w1(1, 1, 1, nc.scalar.copy)
         quantise_w1(1, 1)
-        features(0, 2)
-        features(0, 3)
-        features(1, 0)
-        quantise_x(0, nc.scalar.copy)
-        for t in range(1, PACK):
-            features(1, t)
+        for index in range(2, 2 * PACK):
+            features(index)
+            apply_gain(index - 2)
+            if index - 2 == PACK - 1:
+                nc.vector.tensor_copy(
+                    out=woven[0][:].rearrange("p (c i) t -> p c t i", i=4),
+                    in_=x_rows[:].rearrange("p t (c i) -> p c t i", i=4),
+                )
+            if index == 2 * PACK - 2:
+                quantise_x(0, "wave%d" % index)
+                apply_gain(index)
+        apply_gain(2 * PACK - 1)
 
         sums = [psum.tile([P, M], F32, name="bank%d" % j) for j in range(N // P)]
 
@@ -233,11 +285,16 @@ def tile_list_drift_fence_advisory_kernel(
 
         for j in range(N // P):
             second_product(j, 0)
-        quantise_x(1, nc.vector.tensor_copy)
+        quantise_x(1, "xcodes1")
         for j in range(N // P):
             second_product(j, 1)
             result = keep.tile([P, M], F32, name="result%d" % j)
-            nc.vector.tensor_scalar(
-                out=result[:], in0=sums[j][:], scalar1=least_sb[:, j : j + 1], scalar2=None, op0=ALU.max
-            )
+            if j in (1, 4):
+                above = ring.tile([P, M], F32, name="above")
+                nc.scalar.activation(out=above[:], in_=sums[j][:], func=ACT.Relu, bias=below_sb[:, j : j + 1])
+                nc.scalar.activation(out=result[:], in_=above[:], func=ACT.Identity, bias=least_sb[:, j : j + 1])
+            else:
+                nc.vector.tensor_scalar(
+                    out=result[:], in0=sums[j][:], scalar1=least_sb[:, j : j + 1], scalar2=None, op0=ALU.max
+                )
             nc.sync.dma_start(out=out[P * j : P * (j + 1), :], in_=result[:])

@@ -73,11 +73,11 @@ def tile_list_drift_fence_advisory_kernel(
         tab_sb = []
         w_raw = {}
 
-        def load_table(a):
+        def load_table(a, pieces):
             buf = staged([P, T], U32, 4 * T, "tab%d" % a)
             words = tab_words[a].rearrange("p n i -> p (n i)").bitcast(I32)
-            for c in range(2):
-                cols = slice(T // 2 * c, T // 2 * (c + 1))
+            for c in range(pieces):
+                cols = slice(T // pieces * c, T // pieces * (c + 1))
                 nc.sync.dma_start(out=buf[:, cols].bitcast(I32), in_=words[:, cols])
             tab_sb.append(buf)
 
@@ -100,13 +100,14 @@ def tile_list_drift_fence_advisory_kernel(
         w_codes = {}
         w_scales = {}
 
-        def round_w1(a, b, c, copy):
+        def round_w1(a, b, c, copy, first=0, last=None):
             if (a, b) not in w_bf:
                 w_bf[(a, b)] = keep.tile([P, PACK, P, PACK], BF16, name="wbf%d%d" % (a, b), align_bytes=64)
             per = w_raw[(a, b, c)].shape[2] // PACK
+            last = per if last is None else last
             copy(
-                out=w_bf[(a, b)][:, :, per * c : per * (c + 1), :].rearrange("p t m j -> p m t j"),
-                in_=w_raw[(a, b, c)][:].rearrange("p j (m t) -> p m t j", t=PACK),
+                out=w_bf[(a, b)][:, :, per * c + first : per * c + last, :].rearrange("p t m j -> p m t j"),
+                in_=w_raw[(a, b, c)][:].rearrange("p j (m t) -> p m t j", t=PACK)[:, first:last],
             )
 
         def quantise_w1(a, b, cuts=(0, PACK)):
@@ -121,9 +122,9 @@ def tile_list_drift_fence_advisory_kernel(
             w_codes[(a, b)] = codes
             w_scales[(a, b)] = scales
 
-        load_table(0)
+        load_table(0, 2)
         load_w1(0, 0, 2)
-        load_table(1)
+        load_table(1, 4)
 
         picked_bytes = keep.tile([P, S], U8, align_bytes=64)
         nc.vector.tensor_copy(out=picked_bytes[:], in_=tab_bytes[:].indirect(offs_sb[:]))
@@ -135,7 +136,8 @@ def tile_list_drift_fence_advisory_kernel(
                     out=v_scales[8 * a + 2 + e : P : 32, :].bitcast(I32),
                     in_=picked_bytes[16 + 8 * a + e : P : 32, :].bitcast(I32),
                 )
-        load_w1(1, 0, 4)
+
+        load_w1(1, 0, 2)
 
         v_codes = []
 
@@ -149,8 +151,9 @@ def tile_list_drift_fence_advisory_kernel(
             round_w1(0, 0, c, nc.scalar.copy)
         quantise_w1(0, 0)
         pick_words(1)
-        for c in range(4):
-            round_w1(1, 0, c, nc.scalar.copy if c < 3 else nc.vector.tensor_copy)
+        round_w1(1, 0, 0, nc.scalar.copy)
+        round_w1(1, 0, 1, nc.scalar.copy, 0, 20)
+        round_w1(1, 0, 1, nc.vector.tensor_copy, 20)
         quantise_w1(1, 0, (0, 1, 2, PACK))
 
         shelter_sb = {}
@@ -162,11 +165,12 @@ def tile_list_drift_fence_advisory_kernel(
             shelter_sb[(b, t0)] = buf[:, 0, :]
             shelter_sb[(b, t0 + 1)] = buf[:, 1, :]
 
-        load_w1(0, 1, 2)
+        load_w1(0, 1, 1)
         load_shelter(0, 0)
-        load_w1(1, 1, 2)
+        load_w1(1, 1, 1)
         load_shelter(0, 2)
         load_shelter(1, 0)
+        last_shelter_at = placed[-1]
         load_shelter(1, 2)
         w4_sb = staged([P, 2, 2 * N], U8, 4 * N, "w4_sb")
         for a in range(2):
@@ -181,18 +185,18 @@ def tile_list_drift_fence_advisory_kernel(
             nc.sync.dma_start(out=least_sb[:], in_=least.rearrange("(j p) -> p j", p=P))
 
         round_w1(0, 1, 0, nc.vector.tensor_copy)
-        round_w1(0, 1, 1, nc.vector.tensor_copy)
         quantise_w1(0, 1)
 
         amp_sb = keep.tile([P, 2, PACK], F32)
         nc.vector.tensor_scalar(out=amp_sb[:], in0=gain_sb[:], scalar1=math.sqrt(2.0), scalar2=None, op0=ALU.mult)
         below_sb = keep.tile([P, N // P], F32)
         nc.gpsimd.tensor_scalar(out=below_sb[:], in0=least_sb[:], scalar1=-1.0, scalar2=0.0, op0=ALU.mult, op1=ALU.add)
-        x_rows = keep.tile([P, PACK, M], BF16, align_bytes=64)
+        x_rows = [keep.tile([P, PACK - b, M], BF16, name="xrows%d" % b, align_bytes=64) for b in range(2)]
         woven = [keep.tile([P, M, PACK], BF16, name="woven%d" % b, align_bytes=64) for b in range(2)]
         x_codes = {}
         x_scales = [keep.tile([P, M], U8, name="xscales%d" % b, align_bytes=64) for b in range(2)]
 
+        lees = []
         diffs = []
 
         def features(index):
@@ -201,15 +205,16 @@ def tile_list_drift_fence_advisory_kernel(
             for half in range(2):
                 bank = psum.tile([P, BANK], F32, name="bank%d" % ((2 * index + half) % 8))
                 cols = slice(BANK * half, BANK * (half + 1))
-                for a in range(2):
+                order = (1, 0) if index in (2, 3) else (0, 1)
+                for a in order:
                     nc.tensor.matmul_mx(
                         out=bank[:],
                         lhsT=w_codes[(a, b)][:, P * t : P * (t + 1)].bitcast(FP8X4),
                         lhsT_scale=w_scales[(a, b)][:, P * t : P * (t + 1)],
                         rhs=v_codes[a][:, cols].bitcast(FP8X4),
                         rhs_scale=v_scales[8 * a : P, cols],
-                        start=(a == 0),
-                        stop=(a == 1),
+                        start=(a == order[0]),
+                        stop=(a == order[1]),
                     )
                 nc.scalar.activation(out=folded[:, cols], in_=bank[:], func=ACT.Abs, bias=fold_bias[:])
             wave = keep.tile([P, S], F32, name="wave%d" % index, align_bytes=64)
@@ -218,12 +223,16 @@ def tile_list_drift_fence_advisory_kernel(
                 cols = slice(c0, c0 + width)
                 nc.scalar.activation(out=wave[:, cols], in_=folded[:, cols], func=ACT.Sin, scale=-1.0, bias=wave_bias[:])
             lee = ring.tile([P, M], F32, name="lee")
-            diff = keep.tile([P, M], F32, name="diff%d" % index)
-            diffs.append(diff)
             for h in range(2):
                 cols = slice(HALF * h, HALF * (h + 1))
                 entries = pos2_sb[:, HALF // 16 * h : HALF // 16 * (h + 1)]
                 nc.vector.tensor_tensor(lee[:, cols], wave[:].indirect(entries), shelter_sb[(b, t)][:, cols], ALU.mult)
+            lees.append((wave, lee))
+
+        def differences(index, name):
+            wave, lee = lees[index]
+            diff = keep.tile([P, M], F32, name=name, align_bytes=64)
+            diffs.append(diff)
             for h in range(2):
                 cols = slice(HALF * h, HALF * (h + 1))
                 entries = pos1_sb[:, HALF // 16 * h : HALF // 16 * (h + 1)]
@@ -233,10 +242,8 @@ def tile_list_drift_fence_advisory_kernel(
             b, t = divmod(index, PACK)
             diff = diffs[index]
             factor = amp_sb[:, b, t : t + 1]
-            if b == 0:
-                nc.scalar.activation(out=x_rows[:, t, :], in_=diff[:], func=ACT.Copy, scale=factor)
-            elif t < 2:
-                nc.scalar.activation(out=woven[1][:, :, t], in_=diff[:], func=ACT.Copy, scale=factor)
+            if index < 2 * PACK - 1:
+                nc.scalar.activation(out=x_rows[b][:, t, :], in_=diff[:], func=ACT.Copy, scale=factor)
             else:
                 for h in range(2):
                     cols = slice(HALF * h, HALF * (h + 1))
@@ -244,31 +251,38 @@ def tile_list_drift_fence_advisory_kernel(
                         out=woven[1][:, cols, t], in0=diff[:, cols], scalar1=factor, scalar2=None, op0=ALU.mult
                     )
 
-        def quantise_x(b, name):
-            x_codes[b] = keep.tile([P, M], U32, name=name, align_bytes=64)
+        def weave(b):
+            nc.vector.tensor_copy(
+                out=woven[b][:, :, 0 : PACK - b].rearrange("p (c i) t -> p c t i", i=4),
+                in_=x_rows[b][:].rearrange("p t (c i) -> p c t i", i=4),
+            )
+
+        def quantise_x(b, offset):
+            x_codes[b] = stage.tile([P, M], U32, name="xcodes%d" % b, offset=offset, align_bytes=64)
             nc.vector.quantize_mx(
                 out=x_codes[b][:].bitcast(FP8X4),
                 scales=x_scales[b][:],
                 in_=woven[b][:].rearrange("p m t -> p (m t)"),
             )
 
-        features(0)
-        features(1)
-        round_w1(1, 1, 0, nc.scalar.copy)
-        round_w1(1, 1, 1, nc.scalar.copy)
-        quantise_w1(1, 1)
-        for index in range(2, 2 * PACK):
+        last = 2 * PACK - 1
+        for index in range(last + 1):
             features(index)
-            apply_gain(index - 2)
+            if index < last:
+                differences(index, "diff%d" % index)
+            if index == 1:
+                round_w1(1, 1, 0, nc.scalar.copy, 0, 64)
+                round_w1(1, 1, 0, nc.vector.tensor_copy, 64)
+                quantise_w1(1, 1)
+            if index >= 2:
+                apply_gain(index - 2)
             if index - 2 == PACK - 1:
-                nc.vector.tensor_copy(
-                    out=woven[0][:].rearrange("p (c i) t -> p c t i", i=4),
-                    in_=x_rows[:].rearrange("p t (c i) -> p c t i", i=4),
-                )
-            if index == 2 * PACK - 2:
-                quantise_x(0, "wave%d" % index)
-                apply_gain(index)
-        apply_gain(2 * PACK - 1)
+                weave(0)
+        quantise_x(0, last_shelter_at)
+        apply_gain(last - 1)
+        weave(1)
+        differences(last, "xrows1")
+        apply_gain(last)
 
         sums = [psum.tile([P, M], F32, name="bank%d" % j) for j in range(N // P)]
 
@@ -285,11 +299,11 @@ def tile_list_drift_fence_advisory_kernel(
 
         for j in range(N // P):
             second_product(j, 0)
-        quantise_x(1, "xcodes1")
+        quantise_x(1, last_shelter_at + 4 * M)
         for j in range(N // P):
             second_product(j, 1)
             result = keep.tile([P, M], F32, name="result%d" % j)
-            if j in (1, 4):
+            if j in (1, 3):
                 above = ring.tile([P, M], F32, name="above")
                 nc.scalar.activation(out=above[:], in_=sums[j][:], func=ACT.Relu, bias=below_sb[:, j : j + 1])
                 nc.scalar.activation(out=result[:], in_=above[:], func=ACT.Identity, bias=least_sb[:, j : j + 1])

@@ -81,9 +81,9 @@ def tile_list_drift_fence_advisory_kernel(
                 nc.sync.dma_start(out=buf[:, cols].bitcast(I32), in_=words[:, cols])
             tab_sb.append(buf)
 
-        def load_w1(a, b, pieces):
-            width = PASS // pieces
-            for c in range(pieces):
+        def load_w1(a, b, halves=(0, 1)):
+            width = PASS // 2
+            for c in halves:
                 name = "wraw%d%d%d" % (a, b, c)
                 if (a, b, c) == (0, 0, 0):
                     buf = keep.tile([P, PACK, width], F32, name=name)
@@ -106,8 +106,8 @@ def tile_list_drift_fence_advisory_kernel(
             per = w_raw[(a, b, c)].shape[2] // PACK
             last = per if last is None else last
             copy(
-                out=w_bf[(a, b)][:, :, per * c + first : per * c + last, :].rearrange("p t m j -> p m t j"),
-                in_=w_raw[(a, b, c)][:].rearrange("p j (m t) -> p m t j", t=PACK)[:, first:last],
+                out=w_bf[(a, b)][:, :, per * c + first : per * c + last, :].rearrange("p t m j -> p m j t"),
+                in_=w_raw[(a, b, c)][:].rearrange("p j (m t) -> p m j t", t=PACK)[:, first:last],
             )
 
         def quantise_w1(a, b, cuts=(0, PACK)):
@@ -122,9 +122,9 @@ def tile_list_drift_fence_advisory_kernel(
             w_codes[(a, b)] = codes
             w_scales[(a, b)] = scales
 
-        load_table(0, 2)
-        load_w1(0, 0, 2)
-        load_table(1, 4)
+        load_table(0, 4)
+        load_w1(0, 0)
+        load_table(1, 2)
 
         picked_bytes = keep.tile([P, S], U8, align_bytes=64)
         nc.vector.tensor_copy(out=picked_bytes[:], in_=tab_bytes[:].indirect(offs_sb[:]))
@@ -137,7 +137,7 @@ def tile_list_drift_fence_advisory_kernel(
                     in_=picked_bytes[16 + 8 * a + e : P : 32, :].bitcast(I32),
                 )
 
-        load_w1(1, 0, 2)
+        load_w1(1, 0)
 
         v_codes = []
 
@@ -165,9 +165,10 @@ def tile_list_drift_fence_advisory_kernel(
             shelter_sb[(b, t0)] = buf[:, 0, :]
             shelter_sb[(b, t0 + 1)] = buf[:, 1, :]
 
-        load_w1(0, 1, 1)
+        load_w1(0, 1)
+        load_w1(1, 1, (0,))
         load_shelter(0, 0)
-        load_w1(1, 1, 1)
+        load_w1(1, 1, (1,))
         load_shelter(0, 2)
         load_shelter(1, 0)
         last_shelter_at = placed[-1]
@@ -185,7 +186,9 @@ def tile_list_drift_fence_advisory_kernel(
             nc.sync.dma_start(out=least_sb[:], in_=least.rearrange("(j p) -> p j", p=P))
 
         round_w1(0, 1, 0, nc.vector.tensor_copy)
+        round_w1(0, 1, 1, nc.vector.tensor_copy)
         quantise_w1(0, 1)
+        round_w1(1, 1, 0, nc.vector.tensor_copy)
 
         amp_sb = keep.tile([P, 2, PACK], F32)
         nc.vector.tensor_scalar(out=amp_sb[:], in0=gain_sb[:], scalar1=math.sqrt(2.0), scalar2=None, op0=ALU.mult)
@@ -271,8 +274,7 @@ def tile_list_drift_fence_advisory_kernel(
             if index < last:
                 differences(index, "diff%d" % index)
             if index == 1:
-                round_w1(1, 1, 0, nc.scalar.copy, 0, 64)
-                round_w1(1, 1, 0, nc.vector.tensor_copy, 64)
+                round_w1(1, 1, 1, nc.vector.tensor_copy)
                 quantise_w1(1, 1)
             if index >= 2:
                 apply_gain(index - 2)

@@ -21,8 +21,20 @@ P = 128
 PACK = 4
 PASS = P * PACK
 BANK = 512
-HALF = M // 2
+BANKS = 8
+GROUP = 16
+QUADRANT = 32
+V_PLANE_STEP = 8
+W_HALF = PASS // 2
+W_GROUPS = W_HALF // PACK
+M_HALF = M // 2
+LAST_TILE = H // P - 1
 STAGE_BYTES = 66 * 1024
+SMALL_BYTES = 64
+SCALAR_GROUPS = 20
+GAIN_LAG = 2
+PASS_1_FIRST = (2, 3)
+SCALAR_BLOCKS = (1, 3)
 
 
 def tile_list_drift_fence_advisory_kernel(
@@ -38,37 +50,39 @@ def tile_list_drift_fence_advisory_kernel(
 
         tab_bytes = keep.tile([P, T], U8, align_bytes=64)
         nc.vector.memset(tab_bytes[:].bitcast(I32), 0)
+
         ones = stage.tile([P, STAGE_BYTES // 4], F32, offset=0, align_bytes=64)
         nc.vector.memset(ones[:, 0:1], 1.0)
         fold_bias = keep.tile([P, 1], F32)
         wave_bias = keep.tile([P, 1], F32)
         nc.vector.tensor_scalar(out=fold_bias[:], in0=ones[:, 0:1], scalar1=-math.pi / 4, scalar2=None, op0=ALU.mult)
         nc.vector.tensor_scalar(out=wave_bias[:], in0=ones[:, 0:1], scalar1=math.pi / 2, scalar2=None, op0=ALU.mult)
-        warm_out = keep.tile([P, 1], F32)
-        nc.scalar.activation(out=warm_out[:], in_=wave_bias[:], func=ACT.Sin, bias=fold_bias[:])
+        half_root2 = keep.tile([P, 1], F32)
+        nc.scalar.activation(out=half_root2[:], in_=wave_bias[:], func=ACT.Sin, bias=fold_bias[:])
 
-        placed = [0]
+        stage_ends = [0]
 
         def staged(shape, dtype, size, name):
-            buf = stage.tile(shape, dtype, name=name, offset=placed[-1], align_bytes=64)
-            placed.append(placed[-1] + size)
-            assert placed[-1] <= STAGE_BYTES
+            buf = stage.tile(shape, dtype, name=name, offset=stage_ends[-1], align_bytes=64)
+            stage_ends.append(stage_ends[-1] + size)
+            assert stage_ends[-1] <= STAGE_BYTES
             return buf
 
         w4_sc = staged([P, 2, N], U8, 2 * N, "w4_sc")
         nc.vector.memset(w4_sc[:].rearrange("p a n -> p (a n)").bitcast(I32), 0)
 
-        offs_sb = lists.tile([P, S // 16], U16)
-        pos1_sb = lists.tile([P, M // 16], U16)
-        pos2_sb = lists.tile([P, M // 16], U16)
+        offs_sb = lists.tile([P, S // GROUP], U16)
+        pos1_sb = lists.tile([P, M // GROUP], U16)
+        pos2_sb = lists.tile([P, M // GROUP], U16)
         nc.sync.dma_start(offs_sb[:], offs)
         nc.sync.dma_start(pos2_sb[:], pos2)
         nc.sync.dma_start(pos1_sb[:], pos1)
         gain_sb = keep.tile([P, 2, PACK], F32)
         nc.sync.dma_start(out=gain_sb[:], in_=gain.rearrange("(b p t) -> p b t", b=2, t=PACK))
-        rows = tab_scales.rearrange("a (g e) t -> e g a t", e=2)
+
+        scale_rows = tab_scales.rearrange("a (g e) t -> e g a t", e=2)
         for e in range(2):
-            nc.sync.dma_start(out=tab_bytes[e:P:8, :].bitcast(I32), in_=rows[e].bitcast(I32))
+            nc.sync.dma_start(out=tab_bytes[e:P:V_PLANE_STEP, :].bitcast(I32), in_=scale_rows[e].bitcast(I32))
 
         tab_sb = []
         w_raw = {}
@@ -82,17 +96,16 @@ def tile_list_drift_fence_advisory_kernel(
             tab_sb.append(buf)
 
         def load_w1(a, b, halves=(0, 1)):
-            width = PASS // 2
             for c in halves:
                 name = "wraw%d%d%d" % (a, b, c)
                 if (a, b, c) == (0, 0, 0):
-                    buf = keep.tile([P, PACK, width], F32, name=name)
+                    buf = keep.tile([P, PACK, W_HALF], F32, name=name)
                 else:
-                    buf = staged([P, PACK, width], F32, 4 * PACK * width, name)
-                c0 = PASS * b + width * c
+                    buf = staged([P, PACK, W_HALF], F32, 4 * PACK * W_HALF, name)
+                c0 = PASS * b + W_HALF * c
                 nc.sync.dma_start(
                     out=buf[:],
-                    in_=w1[PASS * a : PASS * (a + 1), c0 : c0 + width].rearrange("(p j) c -> p j c", j=PACK),
+                    in_=w1[PASS * a : PASS * (a + 1), c0 : c0 + W_HALF].rearrange("(p j) c -> p j c", j=PACK),
                 )
                 w_raw[(a, b, c)] = buf
 
@@ -100,14 +113,12 @@ def tile_list_drift_fence_advisory_kernel(
         w_codes = {}
         w_scales = {}
 
-        def round_w1(a, b, c, copy, first=0, last=None):
+        def round_w1(a, b, c, copy, begin=0, end=W_GROUPS):
             if (a, b) not in w_bf:
                 w_bf[(a, b)] = keep.tile([P, PACK, P, PACK], BF16, name="wbf%d%d" % (a, b), align_bytes=64)
-            per = w_raw[(a, b, c)].shape[2] // PACK
-            last = per if last is None else last
             copy(
-                out=w_bf[(a, b)][:, :, per * c + first : per * c + last, :].rearrange("p t m j -> p m j t"),
-                in_=w_raw[(a, b, c)][:].rearrange("p j (m t) -> p m j t", t=PACK)[:, first:last],
+                out=w_bf[(a, b)][:, :, W_GROUPS * c + begin : W_GROUPS * c + end, :].rearrange("p t g j -> p g j t"),
+                in_=w_raw[(a, b, c)][:].rearrange("p j (g t) -> p g j t", t=PACK)[:, begin:end],
             )
 
         def quantise_w1(a, b, cuts=(0, PACK)):
@@ -117,7 +128,7 @@ def tile_list_drift_fence_advisory_kernel(
                 nc.vector.quantize_mx(
                     out=codes[:, P * t0 : P * t1].bitcast(FP8X4),
                     scales=scales[:, P * t0 : P * t1],
-                    in_=w_bf[(a, b)][:, t0:t1].rearrange("p t m j -> p (t m j)"),
+                    in_=w_bf[(a, b)][:, t0:t1].rearrange("p t g j -> p (t g j)"),
                 )
             w_codes[(a, b)] = codes
             w_scales[(a, b)] = scales
@@ -133,8 +144,8 @@ def tile_list_drift_fence_advisory_kernel(
         for a in range(2):
             for e in range(2):
                 nc.sync.dma_start(
-                    out=v_scales[8 * a + 2 + e : P : 32, :].bitcast(I32),
-                    in_=picked_bytes[16 + 8 * a + e : P : 32, :].bitcast(I32),
+                    out=v_scales[V_PLANE_STEP * a + 2 + e : P : QUADRANT, :].bitcast(I32),
+                    in_=picked_bytes[GROUP + V_PLANE_STEP * a + e : P : QUADRANT, :].bitcast(I32),
                 )
 
         load_w1(1, 0)
@@ -152,16 +163,16 @@ def tile_list_drift_fence_advisory_kernel(
         quantise_w1(0, 0)
         pick_words(1)
         round_w1(1, 0, 0, nc.scalar.copy)
-        round_w1(1, 0, 1, nc.scalar.copy, 0, 20)
-        round_w1(1, 0, 1, nc.vector.tensor_copy, 20)
+        round_w1(1, 0, 1, nc.scalar.copy, end=SCALAR_GROUPS)
+        round_w1(1, 0, 1, nc.vector.tensor_copy, begin=SCALAR_GROUPS)
         quantise_w1(1, 0, (0, 1, 2, PACK))
 
         shelter_sb = {}
 
         def load_shelter(b, t0):
             buf = staged([P, 2, M], F32, 8 * M, "shelter%d%d" % (b, t0))
-            rows = shelter[PASS * b : PASS * (b + 1), :].rearrange("(p t) m -> p t m", t=PACK)
-            nc.sync.dma_start(out=buf[:], in_=rows[:, t0 : t0 + 2, :])
+            dealt = shelter[PASS * b : PASS * (b + 1), :].rearrange("(p t) m -> p t m", t=PACK)
+            nc.sync.dma_start(out=buf[:], in_=dealt[:, t0 : t0 + 2, :])
             shelter_sb[(b, t0)] = buf[:, 0, :]
             shelter_sb[(b, t0 + 1)] = buf[:, 1, :]
 
@@ -171,17 +182,17 @@ def tile_list_drift_fence_advisory_kernel(
         load_w1(1, 1, (1,))
         load_shelter(0, 2)
         load_shelter(1, 0)
-        last_shelter_at = placed[-1]
+        last_shelter_at = stage_ends[-1]
         load_shelter(1, 2)
         w4_sb = staged([P, 2, 2 * N], U8, 4 * N, "w4_sb")
         for a in range(2):
             nc.sync.dma_start(out=w4_sb[:, a, :].bitcast(I32), in_=w4_words[a].bitcast(I32))
-        for q in range(4):
+        for d in range(P // QUADRANT):
             nc.sync.dma_start(
-                out=w4_sc[32 * q : 32 * q + 4, :, :].bitcast(I32),
-                in_=w4_scales[:, 4 * q : 4 * q + 4, :].rearrange("a r n -> r a n").bitcast(I32),
+                out=w4_sc[QUADRANT * d : QUADRANT * d + 4, :, :].bitcast(I32),
+                in_=w4_scales[:, 4 * d : 4 * d + 4, :].rearrange("a q n -> q a n").bitcast(I32),
             )
-        least_sb = staged([P, N // P], F32, 64, "least_sb")
+        least_sb = staged([P, N // P], F32, SMALL_BYTES, "least_sb")
         with nc.allow_non_contiguous_dma(reason="one floor for each output row, rows on partitions"):
             nc.sync.dma_start(out=least_sb[:], in_=least.rearrange("(j p) -> p j", p=P))
 
@@ -191,31 +202,43 @@ def tile_list_drift_fence_advisory_kernel(
         round_w1(1, 1, 0, nc.vector.tensor_copy)
 
         amp_sb = keep.tile([P, 2, PACK], F32)
-        nc.vector.tensor_scalar(out=amp_sb[:], in0=gain_sb[:], scalar1=math.sqrt(2.0), scalar2=None, op0=ALU.mult)
-        below_sb = keep.tile([P, N // P], F32)
-        nc.gpsimd.tensor_scalar(out=below_sb[:], in0=least_sb[:], scalar1=-1.0, scalar2=0.0, op0=ALU.mult, op1=ALU.add)
+        nc.vector.tensor_scalar(
+            out=amp_sb[:], in0=gain_sb[:], scalar1=half_root2[:], scalar2=2.0, op0=ALU.mult, op1=ALU.mult
+        )
+        minus_least = keep.tile([P, N // P], F32)
+        nc.gpsimd.tensor_scalar(
+            out=minus_least[:], in0=least_sb[:], scalar1=-1.0, scalar2=0.0, op0=ALU.mult, op1=ALU.add
+        )
+
         x_rows = [keep.tile([P, PACK - b, M], BF16, name="xrows%d" % b, align_bytes=64) for b in range(2)]
         woven = [keep.tile([P, M, PACK], BF16, name="woven%d" % b, align_bytes=64) for b in range(2)]
         x_codes = {}
         x_scales = [keep.tile([P, M], U8, name="xscales%d" % b, align_bytes=64) for b in range(2)]
 
+        waves = []
         lees = []
         diffs = []
+
+        def gather_halves(result, wave, pos_sb, other, op):
+            for h in range(2):
+                cols = slice(M_HALF * h, M_HALF * (h + 1))
+                entries = pos_sb[:, M_HALF // GROUP * h : M_HALF // GROUP * (h + 1)]
+                nc.vector.tensor_tensor(result[:, cols], wave[:].indirect(entries), other[:, cols], op)
 
         def features(index):
             b, t = divmod(index, PACK)
             folded = ring.tile([P, S], F32, name="folded")
-            for half in range(2):
-                bank = psum.tile([P, BANK], F32, name="bank%d" % ((2 * index + half) % 8))
+            order = (1, 0) if index in PASS_1_FIRST else (0, 1)
+            for half in range(S // BANK):
+                bank = psum.tile([P, BANK], F32, name="bank%d" % ((2 * index + half) % BANKS))
                 cols = slice(BANK * half, BANK * (half + 1))
-                order = (1, 0) if index in (2, 3) else (0, 1)
                 for a in order:
                     nc.tensor.matmul_mx(
                         out=bank[:],
                         lhsT=w_codes[(a, b)][:, P * t : P * (t + 1)].bitcast(FP8X4),
                         lhsT_scale=w_scales[(a, b)][:, P * t : P * (t + 1)],
                         rhs=v_codes[a][:, cols].bitcast(FP8X4),
-                        rhs_scale=v_scales[8 * a : P, cols],
+                        rhs_scale=v_scales[V_PLANE_STEP * a : P, cols],
                         start=(a == order[0]),
                         stop=(a == order[1]),
                     )
@@ -226,38 +249,31 @@ def tile_list_drift_fence_advisory_kernel(
                 cols = slice(c0, c0 + width)
                 nc.scalar.activation(out=wave[:, cols], in_=folded[:, cols], func=ACT.Sin, scale=-1.0, bias=wave_bias[:])
             lee = ring.tile([P, M], F32, name="lee")
-            for h in range(2):
-                cols = slice(HALF * h, HALF * (h + 1))
-                entries = pos2_sb[:, HALF // 16 * h : HALF // 16 * (h + 1)]
-                nc.vector.tensor_tensor(lee[:, cols], wave[:].indirect(entries), shelter_sb[(b, t)][:, cols], ALU.mult)
-            lees.append((wave, lee))
+            gather_halves(lee, wave, pos2_sb, shelter_sb[(b, t)], ALU.mult)
+            waves.append(wave)
+            lees.append(lee)
 
         def differences(index, name):
-            wave, lee = lees[index]
             diff = keep.tile([P, M], F32, name=name, align_bytes=64)
+            gather_halves(diff, waves[index], pos1_sb, lees[index], ALU.subtract)
             diffs.append(diff)
-            for h in range(2):
-                cols = slice(HALF * h, HALF * (h + 1))
-                entries = pos1_sb[:, HALF // 16 * h : HALF // 16 * (h + 1)]
-                nc.vector.tensor_tensor(diff[:, cols], wave[:].indirect(entries), lee[:, cols], ALU.subtract)
 
         def apply_gain(index):
             b, t = divmod(index, PACK)
             diff = diffs[index]
             factor = amp_sb[:, b, t : t + 1]
-            if index < 2 * PACK - 1:
+            if index < LAST_TILE:
                 nc.scalar.activation(out=x_rows[b][:, t, :], in_=diff[:], func=ACT.Copy, scale=factor)
             else:
-                for h in range(2):
-                    cols = slice(HALF * h, HALF * (h + 1))
-                    nc.vector.tensor_scalar(
-                        out=woven[1][:, cols, t], in0=diff[:, cols], scalar1=factor, scalar2=None, op0=ALU.mult
-                    )
+                nc.scalar.activation(out=woven[b][:, :M_HALF, t], in_=diff[:, :M_HALF], func=ACT.Copy, scale=factor)
+                nc.vector.tensor_scalar(
+                    out=woven[b][:, M_HALF:, t], in0=diff[:, M_HALF:], scalar1=factor, scalar2=None, op0=ALU.mult
+                )
 
-        def weave(b):
-            nc.vector.tensor_copy(
-                out=woven[b][:, :, 0 : PACK - b].rearrange("p (c i) t -> p c t i", i=4),
-                in_=x_rows[b][:].rearrange("p t (c i) -> p c t i", i=4),
+        def weave(b, cols, copy):
+            copy(
+                out=woven[b][:, cols, 0 : PACK - b].rearrange("p (c i) t -> p c t i", i=4),
+                in_=x_rows[b][:, :, cols].rearrange("p t (c i) -> p c t i", i=4),
             )
 
         def quantise_x(b, offset):
@@ -268,35 +284,35 @@ def tile_list_drift_fence_advisory_kernel(
                 in_=woven[b][:].rearrange("p m t -> p (m t)"),
             )
 
-        last = 2 * PACK - 1
-        for index in range(last + 1):
+        for index in range(LAST_TILE + 1):
             features(index)
-            if index < last:
+            if index < LAST_TILE:
                 differences(index, "diff%d" % index)
             if index == 1:
                 round_w1(1, 1, 1, nc.vector.tensor_copy)
                 quantise_w1(1, 1)
-            if index >= 2:
-                apply_gain(index - 2)
-            if index - 2 == PACK - 1:
-                weave(0)
+            if index >= GAIN_LAG:
+                apply_gain(index - GAIN_LAG)
+            if index - GAIN_LAG == PACK - 1:
+                weave(0, slice(0, M), nc.vector.tensor_copy)
         quantise_x(0, last_shelter_at)
-        apply_gain(last - 1)
-        weave(1)
-        differences(last, "xrows1")
-        apply_gain(last)
+        apply_gain(LAST_TILE - 1)
+        weave(1, slice(0, M_HALF), nc.scalar.copy)
+        weave(1, slice(M_HALF, M), nc.vector.tensor_copy)
+        differences(LAST_TILE, "xrows1")
+        apply_gain(LAST_TILE)
 
         sums = [psum.tile([P, M], F32, name="bank%d" % j) for j in range(N // P)]
 
-        def second_product(j, a):
+        def second_product(j, b):
             nc.tensor.matmul_mx(
                 out=sums[j][:],
-                lhsT=w4_sb[:, a, 2 * P * j : 2 * P * (j + 1)].bitcast(FP4X4),
-                lhsT_scale=w4_sc[:, a, P * j : P * (j + 1)],
-                rhs=x_codes[a][:].bitcast(FP8X4),
-                rhs_scale=x_scales[a][:],
-                start=(a == 0),
-                stop=(a == 1),
+                lhsT=w4_sb[:, b, 2 * P * j : 2 * P * (j + 1)].bitcast(FP4X4),
+                lhsT_scale=w4_sc[:, b, P * j : P * (j + 1)],
+                rhs=x_codes[b][:].bitcast(FP8X4),
+                rhs_scale=x_scales[b][:],
+                start=(b == 0),
+                stop=(b == 1),
             )
 
         for j in range(N // P):
@@ -304,13 +320,13 @@ def tile_list_drift_fence_advisory_kernel(
         quantise_x(1, last_shelter_at + 4 * M)
         for j in range(N // P):
             second_product(j, 1)
-            result = keep.tile([P, M], F32, name="result%d" % j)
-            if j in (1, 3):
+            floored = keep.tile([P, M], F32, name="floored%d" % j)
+            if j in SCALAR_BLOCKS:
                 above = ring.tile([P, M], F32, name="above")
-                nc.scalar.activation(out=above[:], in_=sums[j][:], func=ACT.Relu, bias=below_sb[:, j : j + 1])
-                nc.scalar.activation(out=result[:], in_=above[:], func=ACT.Identity, bias=least_sb[:, j : j + 1])
+                nc.scalar.activation(out=above[:], in_=sums[j][:], func=ACT.Relu, bias=minus_least[:, j : j + 1])
+                nc.scalar.activation(out=floored[:], in_=above[:], func=ACT.Identity, bias=least_sb[:, j : j + 1])
             else:
                 nc.vector.tensor_scalar(
-                    out=result[:], in0=sums[j][:], scalar1=least_sb[:, j : j + 1], scalar2=None, op0=ALU.max
+                    out=floored[:], in0=sums[j][:], scalar1=least_sb[:, j : j + 1], scalar2=None, op0=ALU.max
                 )
-            nc.sync.dma_start(out=out[P * j : P * (j + 1), :], in_=result[:])
+            nc.sync.dma_start(out=out[P * j : P * (j + 1), :], in_=floored[:])

import math
from contextlib import ExitStack

import concourse.mybir as mybir

K, T, S, H, M, N = 1024, 2048, 1024, 1024, 512, 768
FLOPS = 2 * K * H * S + 2 * H * N * M

F32 = mybir.dt.float32
BF16 = mybir.dt.bfloat16
I32 = mybir.dt.int32
U32 = mybir.dt.uint32
U16 = mybir.dt.uint16
U8 = mybir.dt.uint8
FP8X4 = mybir.dt.float8_e4m3fn_x4
FP4X4 = mybir.dt.float4_e2m1fn_x4
ALU = mybir.AluOpType
ACT = mybir.ActivationFunctionType

P = 128
PACK = 4
PASS = P * PACK
BANK = 512
BANKS = 8
GROUP = 16
QUADRANT = 32
V_PLANE_STEP = 8
W_HALF = PASS // 2
W_GROUPS = W_HALF // PACK
M_HALF = M // 2
LAST_TILE = H // P - 1
STAGE_BYTES = 66 * 1024
SMALL_BYTES = 64
SCALAR_GROUPS = 20
GAIN_LAG = 2
PASS_1_FIRST = (2, 3)
SCALAR_BLOCKS = (1, 3)


def tile_list_drift_fence_advisory_kernel(
    tc, tab_words, tab_scales, offs, w1, gain, pos1, pos2, shelter, w4_words, w4_scales, least, out
):
    nc = tc.nc
    with ExitStack() as ctx:
        lists = ctx.enter_context(tc.tile_pool(name="lists", bufs=1))
        keep = ctx.enter_context(tc.tile_pool(name="keep", bufs=1))
        stage = ctx.enter_context(tc.tile_pool(name="stage", bufs=1))
        ring = ctx.enter_context(tc.tile_pool(name="ring", bufs=2))
        psum = ctx.enter_context(tc.psum_pool(name="psum", bufs=1))

        tab_bytes = keep.tile([P, T], U8, align_bytes=64)
        nc.vector.memset(tab_bytes[:].bitcast(I32), 0)

        ones = stage.tile([P, STAGE_BYTES // 4], F32, offset=0, align_bytes=64)
        nc.vector.memset(ones[:, 0:1], 1.0)
        fold_bias = keep.tile([P, 1], F32)
        wave_bias = keep.tile([P, 1], F32)
        nc.vector.tensor_scalar(out=fold_bias[:], in0=ones[:, 0:1], scalar1=-math.pi / 4, scalar2=None, op0=ALU.mult)
        nc.vector.tensor_scalar(out=wave_bias[:], in0=ones[:, 0:1], scalar1=math.pi / 2, scalar2=None, op0=ALU.mult)
        half_root2 = keep.tile([P, 1], F32)
        nc.scalar.activation(out=half_root2[:], in_=wave_bias[:], func=ACT.Sin, bias=fold_bias[:])

        stage_ends = [0]

        def staged(shape, dtype, size, name):
            buf = stage.tile(shape, dtype, name=name, offset=stage_ends[-1], align_bytes=64)
            stage_ends.append(stage_ends[-1] + size)
            assert stage_ends[-1] <= STAGE_BYTES
            return buf

        w4_sc = staged([P, 2, N], U8, 2 * N, "w4_sc")
        nc.vector.memset(w4_sc[:].rearrange("p a n -> p (a n)").bitcast(I32), 0)

        offs_sb = lists.tile([P, S // GROUP], U16)
        pos1_sb = lists.tile([P, M // GROUP], U16)
        pos2_sb = lists.tile([P, M // GROUP], U16)
        nc.sync.dma_start(offs_sb[:], offs)
        nc.sync.dma_start(pos2_sb[:], pos2)
        nc.sync.dma_start(pos1_sb[:], pos1)
        gain_sb = keep.tile([P, 2, PACK], F32)
        nc.sync.dma_start(out=gain_sb[:], in_=gain.rearrange("(b p t) -> p b t", b=2, t=PACK))

        scale_rows = tab_scales.rearrange("a (g e) t -> e g a t", e=2)
        for e in range(2):
            nc.sync.dma_start(out=tab_bytes[e:P:V_PLANE_STEP, :].bitcast(I32), in_=scale_rows[e].bitcast(I32))

        tab_sb = []
        w_raw = {}

        def load_table(a, pieces):
            buf = staged([P, T], U32, 4 * T, "tab%d" % a)
            words = tab_words[a].rearrange("p n i -> p (n i)").bitcast(I32)
            for c in range(pieces):
                cols = slice(T // pieces * c, T // pieces * (c + 1))
                nc.sync.dma_start(out=buf[:, cols].bitcast(I32), in_=words[:, cols])
            tab_sb.append(buf)

        def load_w1(a, b, halves=(0, 1)):
            for c in halves:
                name = "wraw%d%d%d" % (a, b, c)
                if (a, b, c) == (0, 0, 0):
                    buf = keep.tile([P, PACK, W_HALF], F32, name=name)
                else:
                    buf = staged([P, PACK, W_HALF], F32, 4 * PACK * W_HALF, name)
                c0 = PASS * b + W_HALF * c
                nc.sync.dma_start(
                    out=buf[:],
                    in_=w1[PASS * a : PASS * (a + 1), c0 : c0 + W_HALF].rearrange("(p j) c -> p j c", j=PACK),
                )
                w_raw[(a, b, c)] = buf

        w_bf = {}
        w_codes = {}
        w_scales = {}

        def round_w1(a, b, c, copy, begin=0, end=W_GROUPS):
            if (a, b) not in w_bf:
                w_bf[(a, b)] = keep.tile([P, PACK, P, PACK], BF16, name="wbf%d%d" % (a, b), align_bytes=64)
            copy(
                out=w_bf[(a, b)][:, :, W_GROUPS * c + begin : W_GROUPS * c + end, :].rearrange("p t g j -> p g j t"),
                in_=w_raw[(a, b, c)][:].rearrange("p j (g t) -> p g j t", t=PACK)[:, begin:end],
            )

        def quantise_w1(a, b, cuts=(0, PACK)):
            codes = keep.tile([P, PASS], U32, name="wcodes%d%d" % (a, b), align_bytes=64)
            scales = keep.tile([P, PASS], U8, name="wscales%d%d" % (a, b), align_bytes=64)
            for t0, t1 in zip(cuts[:-1], cuts[1:]):
                nc.vector.quantize_mx(
                    out=codes[:, P * t0 : P * t1].bitcast(FP8X4),
                    scales=scales[:, P * t0 : P * t1],
                    in_=w_bf[(a, b)][:, t0:t1].rearrange("p t g j -> p (t g j)"),
                )
            w_codes[(a, b)] = codes
            w_scales[(a, b)] = scales

        load_table(0, 4)
        load_w1(0, 0)
        load_table(1, 2)

        picked_bytes = keep.tile([P, S], U8, align_bytes=64)
        nc.vector.tensor_copy(out=picked_bytes[:], in_=tab_bytes[:].indirect(offs_sb[:]))
        v_scales = keep.tile([P, S], U8, align_bytes=64)
        nc.vector.tensor_copy(out=v_scales[:].bitcast(I32), in_=picked_bytes[:].bitcast(I32))
        for a in range(2):
            for e in range(2):
                nc.sync.dma_start(
                    out=v_scales[V_PLANE_STEP * a + 2 + e : P : QUADRANT, :].bitcast(I32),
                    in_=picked_bytes[GROUP + V_PLANE_STEP * a + e : P : QUADRANT, :].bitcast(I32),
                )

        load_w1(1, 0)

        v_codes = []

        def pick_words(a):
            picked = keep.tile([P, S], U32, name="picked%d" % a, align_bytes=64)
            nc.vector.tensor_copy(out=picked[:], in_=tab_sb[a][:].indirect(offs_sb[:]))
            v_codes.append(picked)

        pick_words(0)
        for c in range(2):
            round_w1(0, 0, c, nc.scalar.copy)
        quantise_w1(0, 0)
        pick_words(1)
        round_w1(1, 0, 0, nc.scalar.copy)
        round_w1(1, 0, 1, nc.scalar.copy, end=SCALAR_GROUPS)
        round_w1(1, 0, 1, nc.vector.tensor_copy, begin=SCALAR_GROUPS)
        quantise_w1(1, 0, (0, 1, 2, PACK))

        shelter_sb = {}

        def load_shelter(b, t0):
            buf = staged([P, 2, M], F32, 8 * M, "shelter%d%d" % (b, t0))
            dealt = shelter[PASS * b : PASS * (b + 1), :].rearrange("(p t) m -> p t m", t=PACK)
            nc.sync.dma_start(out=buf[:], in_=dealt[:, t0 : t0 + 2, :])
            shelter_sb[(b, t0)] = buf[:, 0, :]
            shelter_sb[(b, t0 + 1)] = buf[:, 1, :]

        load_w1(0, 1)
        load_w1(1, 1, (0,))
        load_shelter(0, 0)
        load_w1(1, 1, (1,))
        load_shelter(0, 2)
        load_shelter(1, 0)
        last_shelter_at = stage_ends[-1]
        load_shelter(1, 2)
        w4_sb = staged([P, 2, 2 * N], U8, 4 * N, "w4_sb")
        for a in range(2):
            nc.sync.dma_start(out=w4_sb[:, a, :].bitcast(I32), in_=w4_words[a].bitcast(I32))
        for d in range(P // QUADRANT):
            nc.sync.dma_start(
                out=w4_sc[QUADRANT * d : QUADRANT * d + 4, :, :].bitcast(I32),
                in_=w4_scales[:, 4 * d : 4 * d + 4, :].rearrange("a q n -> q a n").bitcast(I32),
            )
        least_sb = staged([P, N // P], F32, SMALL_BYTES, "least_sb")
        with nc.allow_non_contiguous_dma(reason="one floor for each output row, rows on partitions"):
            nc.sync.dma_start(out=least_sb[:], in_=least.rearrange("(j p) -> p j", p=P))

        round_w1(0, 1, 0, nc.vector.tensor_copy)
        round_w1(0, 1, 1, nc.vector.tensor_copy)
        quantise_w1(0, 1)
        round_w1(1, 1, 0, nc.vector.tensor_copy)

        amp_sb = keep.tile([P, 2, PACK], F32)
        nc.vector.tensor_scalar(
            out=amp_sb[:], in0=gain_sb[:], scalar1=half_root2[:], scalar2=2.0, op0=ALU.mult, op1=ALU.mult
        )
        minus_least = keep.tile([P, N // P], F32)
        nc.gpsimd.tensor_scalar(
            out=minus_least[:], in0=least_sb[:], scalar1=-1.0, scalar2=0.0, op0=ALU.mult, op1=ALU.add
        )

        x_rows = [keep.tile([P, PACK - b, M], BF16, name="xrows%d" % b, align_bytes=64) for b in range(2)]
        woven = [keep.tile([P, M, PACK], BF16, name="woven%d" % b, align_bytes=64) for b in range(2)]
        x_codes = {}
        x_scales = [keep.tile([P, M], U8, name="xscales%d" % b, align_bytes=64) for b in range(2)]

        waves = []
        lees = []
        diffs = []

        def gather_halves(result, wave, pos_sb, other, op):
            for h in range(2):
                cols = slice(M_HALF * h, M_HALF * (h + 1))
                entries = pos_sb[:, M_HALF // GROUP * h : M_HALF // GROUP * (h + 1)]
                nc.vector.tensor_tensor(result[:, cols], wave[:].indirect(entries), other[:, cols], op)

        def features(index):
            b, t = divmod(index, PACK)
            folded = ring.tile([P, S], F32, name="folded")
            order = (1, 0) if index in PASS_1_FIRST else (0, 1)
            for half in range(S // BANK):
                bank = psum.tile([P, BANK], F32, name="bank%d" % ((2 * index + half) % BANKS))
                cols = slice(BANK * half, BANK * (half + 1))
                for a in order:
                    nc.tensor.matmul_mx(
                        out=bank[:],
                        lhsT=w_codes[(a, b)][:, P * t : P * (t + 1)].bitcast(FP8X4),
                        lhsT_scale=w_scales[(a, b)][:, P * t : P * (t + 1)],
                        rhs=v_codes[a][:, cols].bitcast(FP8X4),
                        rhs_scale=v_scales[V_PLANE_STEP * a : P, cols],
                        start=(a == order[0]),
                        stop=(a == order[1]),
                    )
                nc.scalar.activation(out=folded[:, cols], in_=bank[:], func=ACT.Abs, bias=fold_bias[:])
            wave = keep.tile([P, S], F32, name="wave%d" % index, align_bytes=64)
            width = BANK if index == 0 else S
            for c0 in range(0, S, width):
                cols = slice(c0, c0 + width)
                nc.scalar.activation(out=wave[:, cols], in_=folded[:, cols], func=ACT.Sin, scale=-1.0, bias=wave_bias[:])
            lee = ring.tile([P, M], F32, name="lee")
            gather_halves(lee, wave, pos2_sb, shelter_sb[(b, t)], ALU.mult)
            waves.append(wave)
            lees.append(lee)

        def differences(index, name):
            diff = keep.tile([P, M], F32, name=name, align_bytes=64)
            gather_halves(diff, waves[index], pos1_sb, lees[index], ALU.subtract)
            diffs.append(diff)

        def apply_gain(index):
            b, t = divmod(index, PACK)
            diff = diffs[index]
            factor = amp_sb[:, b, t : t + 1]
            if index < LAST_TILE:
                nc.scalar.activation(out=x_rows[b][:, t, :], in_=diff[:], func=ACT.Copy, scale=factor)
            else:
                nc.scalar.activation(out=woven[b][:, :M_HALF, t], in_=diff[:, :M_HALF], func=ACT.Copy, scale=factor)
                nc.vector.tensor_scalar(
                    out=woven[b][:, M_HALF:, t], in0=diff[:, M_HALF:], scalar1=factor, scalar2=None, op0=ALU.mult
                )

        def weave(b, cols, copy):
            copy(
                out=woven[b][:, cols, 0 : PACK - b].rearrange("p (c i) t -> p c t i", i=4),
                in_=x_rows[b][:, :, cols].rearrange("p t (c i) -> p c t i", i=4),
            )

        def quantise_x(b, offset):
            x_codes[b] = stage.tile([P, M], U32, name="xcodes%d" % b, offset=offset, align_bytes=64)
            nc.vector.quantize_mx(
                out=x_codes[b][:].bitcast(FP8X4),
                scales=x_scales[b][:],
                in_=woven[b][:].rearrange("p m t -> p (m t)"),
            )

        for index in range(LAST_TILE + 1):
            features(index)
            if index < LAST_TILE:
                differences(index, "diff%d" % index)
            if index == 1:
                round_w1(1, 1, 1, nc.vector.tensor_copy)
                quantise_w1(1, 1)
            if index >= GAIN_LAG:
                apply_gain(index - GAIN_LAG)
            if index - GAIN_LAG == PACK - 1:
                weave(0, slice(0, M), nc.vector.tensor_copy)
        quantise_x(0, last_shelter_at)
        apply_gain(LAST_TILE - 1)
        weave(1, slice(0, M_HALF), nc.scalar.copy)
        weave(1, slice(M_HALF, M), nc.vector.tensor_copy)
        differences(LAST_TILE, "xrows1")
        apply_gain(LAST_TILE)

        sums = [psum.tile([P, M], F32, name="bank%d" % j) for j in range(N // P)]

        def second_product(j, b):
            nc.tensor.matmul_mx(
                out=sums[j][:],
                lhsT=w4_sb[:, b, 2 * P * j : 2 * P * (j + 1)].bitcast(FP4X4),
                lhsT_scale=w4_sc[:, b, P * j : P * (j + 1)],
                rhs=x_codes[b][:].bitcast(FP8X4),
                rhs_scale=x_scales[b][:],
                start=(b == 0),
                stop=(b == 1),
            )

        for j in range(N // P):
            second_product(j, 0)
        quantise_x(1, last_shelter_at + 4 * M)
        for j in range(N // P):
            second_product(j, 1)
            floored = keep.tile([P, M], F32, name="floored%d" % j)
            if j in SCALAR_BLOCKS:
                above = ring.tile([P, M], F32, name="above")
                nc.scalar.activation(out=above[:], in_=sums[j][:], func=ACT.Relu, bias=minus_least[:, j : j + 1])
                nc.scalar.activation(out=floored[:], in_=above[:], func=ACT.Identity, bias=least_sb[:, j : j + 1])
            else:
                nc.vector.tensor_scalar(
                    out=floored[:], in0=sums[j][:], scalar1=least_sb[:, j : j + 1], scalar2=None, op0=ALU.max
                )
            nc.sync.dma_start(out=out[P * j : P * (j + 1), :], in_=floored[:])
